import numpy as np
import ml_dtypes


def mxq(x, axis, fmt="e4m3"):
    dtype, down = {"e4m3": (ml_dtypes.float8_e4m3fn, 7), "e5m2": (ml_dtypes.float8_e5m2, 14)}[fmt]
    v = np.moveaxis(np.asarray(x, np.float32).astype(ml_dtypes.bfloat16).astype(np.float64), axis, -1)
    blocks = v.reshape(v.shape[:-1] + (-1, 32))
    amax = np.abs(blocks).max(-1, keepdims=True)
    byte = np.maximum(np.where(amax > 0, np.frexp(amax)[1] - 1 + 127, 0) - down, 1)
    scale = np.exp2(byte - 127.0)
    codes = (blocks / scale).astype(np.float32).astype(dtype).astype(np.float64)
    return np.moveaxis((codes * scale).reshape(v.shape), -1, axis)


WIDE = False


def mx_kscale(k):
    if not WIDE:
        return np.ones(k)
    levels = np.array([30, -30])
    if k % 512:
        return np.exp2(np.random.permutation(np.resize(levels, k // 32))).repeat(32)
    a = np.empty((k // 512, 16))
    for p in range(k // 512):
        a[p, :8] = np.random.permutation(np.resize(levels, 8))
        for g in range(8):
            far = levels[np.abs(levels - a[p, g]) >= 10]
            a[p, g + 8] = far[np.random.randint(len(far))]
    return np.exp2(a.ravel()).repeat(32)


BF16 = ml_dtypes.bfloat16


def bf(x):
    return np.asarray(x, np.float32).astype(BF16)


def f64(x):
    return np.asarray(x).astype(np.float64)


U, K, D = 2048, 1024, 512


def setup_inputs():
    s, t = mx_kscale(K), mx_kscale(K)
    tail = np.exp(0.5 * np.random.standard_normal((U, K)))
    return {"sim_grad": bf(np.random.standard_normal((U, K)) * tail / np.sqrt(K) * s),
            "cen": bf(np.random.standard_normal((K, D)) / s[:, None]),
            "avg": bf(np.random.random_sample((K, U)) * 2.0 / U * t[:, None]),
            "cen_grad": bf(np.random.standard_normal((K, D)) * U / 2.0 * np.sqrt(3.0 / K) / t[:, None]),
            "emb": bf(np.random.standard_normal((U, D)) / np.sqrt(D)),
            "radial": bf(3.0 * np.random.standard_normal(U)),
            "inv_norm": bf(1.0 + 0.1 * np.random.standard_normal(U))}


def reference(sim_grad, cen, avg, cen_grad, emb, radial, inv_norm):
    direct = mxq(f64(sim_grad), 1, "e5m2") @ mxq(f64(cen), 0, "e4m3")
    shared = mxq(f64(avg), 0, "e4m3").T @ mxq(f64(cen_grad), 0, "e4m3")
    g = direct + shared
    return f64(inv_norm)[:, None] * (g - f64(radial)[:, None] * f64(emb))

@@ -1,0 +1,248 @@
+from contextlib import ExitStack
+
+import concourse.mybir as mybir
+from concourse.masks import make_identity
+
+U, K, D = 2048, 1024, 512
+FLOPS = 2 * 2 * U * K * D
+
+F32 = mybir.dt.float32
+BF16 = mybir.dt.bfloat16
+U32 = mybir.dt.uint32
+U8 = mybir.dt.uint8
+E4M3 = mybir.dt.float8_e4m3fn_x4
+E5M2 = mybir.dt.float8_e5m2_x4
+ALU = mybir.AluOpType
+ACT = mybir.ActivationFunctionType
+
+P = 128
+PACK = 4
+K_PASS = P * PACK
+PASSES = K // K_PASS
+TILES = U // P
+PAIR = 2 * P
+PAIRS = U // PAIR
+CHUNK = 2 * PAIR
+RUN = 4
+CEN_SPLIT = 288
+AVG_SPLIT = 64
+
+
+def interleave(copy, grouped, raw, c0, c1):
+    copy(
+        out=grouped[:, c0:c1, :].rearrange("p (c i) t -> p c t i", i=RUN),
+        in_=raw[:, :, c0:c1].rearrange("p t (c i) -> p c t i", i=RUN),
+    )
+
+
+def tile_ge2e_embedding_gradient_s2_kernel(tc, sim_grad, cen, avg, cen_grad, emb, radial, inv_norm, out):
+    nc = tc.nc
+    with ExitStack() as ctx:
+        keep = ctx.enter_context(tc.tile_pool(name="keep", bufs=1))
+        work = ctx.enter_context(tc.tile_pool(name="work", bufs=3))
+        turn = ctx.enter_context(tc.psum_pool(name="turn", bufs=4))
+        sums = ctx.enter_context(tc.psum_pool(name="sums", bufs=4))
+        ctx.enter_context(tc.manual_schedule())
+
+        sg_raw, emb_raw, avg_raw, w_raw = {}, {}, {}, {}
+
+        def load_sg(s):
+            sg_raw[s] = keep.tile([P, 2, K], BF16, name="sg_raw%d" % s)
+            nc.sync.dma_start(out=sg_raw[s][:], in_=sim_grad[s * PAIR : (s + 1) * PAIR, :].rearrange("(i p) k -> p i k", p=P))
+
+        def load_w(name, w, g):
+            w_raw[name, g] = keep.tile([P, PACK, D], BF16, name="%s_raw%d" % (name, g))
+            nc.sync.dma_start(out=w_raw[name, g][:], in_=w[g * K_PASS : (g + 1) * K_PASS, :].rearrange("(p t) d -> p t d", t=PACK))
+
+        def load_avg(c, g):
+            avg_raw[c, g] = keep.tile([P, PACK, CHUNK], BF16, name="avg_raw%d_%d" % (c, g))
+            rows = avg[g * K_PASS : (g + 1) * K_PASS, c * CHUNK : (c + 1) * CHUNK]
+            nc.sync.dma_start(out=avg_raw[c, g][:], in_=rows.rearrange("(p t) u -> p t u", t=PACK))
+
+        def load_emb(c):
+            emb_raw[c] = keep.tile([P, CHUNK // P, D], BF16, name="emb_raw%d" % c)
+            nc.sync.dma_start(out=emb_raw[c][:], in_=emb[c * CHUNK : (c + 1) * CHUNK, :].rearrange("(i p) d -> p i d", p=P))
+
+        vec_raw = keep.tile([2 * TILES, P], BF16)
+        load_w("cen", cen, 0)
+        load_sg(0)
+        load_w("cen", cen, 1)
+        load_sg(1)
+        nc.sync.dma_start(out=vec_raw[0:TILES, :], in_=radial.rearrange("(i p) -> i p", p=P))
+        nc.sync.dma_start(out=vec_raw[TILES : 2 * TILES, :], in_=inv_norm.rearrange("(i p) -> i p", p=P))
+        load_w("cen_grad", cen_grad, 0)
+        load_avg(0, 0)
+        load_w("cen_grad", cen_grad, 1)
+        load_avg(0, 1)
+        for c in range(U // CHUNK):
+            if c > 0:
+                load_avg(c, 0)
+                load_avg(c, 1)
+                load_sg(2 * c + 1)
+            if 2 * c + 2 < PAIRS:
+                load_sg(2 * c + 2)
+            load_emb(c)
+
+        ident = keep.tile([P, P], F32)
+        make_identity(nc, ident[:])
+        vec_rows = keep.tile([P, P], F32)
+        nc.scalar.copy(out=vec_rows[:], in_=ident[:])
+        vec_cols = keep.tile([P, 2 * TILES], F32)
+        rad_inv = keep.tile([P, TILES], F32)
+
+        w_codes, w_scales, w_grouped = {}, {}, {}
+        banks, sg_grouped, avg_grouped, sg_q, avg_q, acc, res, rad_emb = {}, {}, {}, {}, {}, {}, {}, {}
+
+        def w_interleave(name, g):
+            w_grouped[name, g] = keep.tile([P, D, PACK], BF16, name="%s_grouped%d" % (name, g), align_bytes=64)
+            interleave(nc.vector.tensor_copy, w_grouped[name, g], w_raw[name, g], 0, CEN_SPLIT)
+            interleave(nc.scalar.copy, w_grouped[name, g], w_raw[name, g], CEN_SPLIT, D)
+
+        def w_quantize(name, g):
+            w_codes[name, g] = keep.tile([P, D], U32, name="%s_codes%d" % (name, g), align_bytes=64)
+            w_scales[name, g] = keep.tile([P, D], U8, name="%s_scales%d" % (name, g), align_bytes=64)
+            nc.vector.quantize_mx(
+                out=w_codes[name, g][:].bitcast(E4M3),
+                scales=w_scales[name, g][:],
+                in_=w_grouped[name, g][:].rearrange("p d t -> p (d t)"),
+            )
+
+        def sg_transpose(s):
+            for i in range(2):
+                bank = turn.tile([P, PASSES, 2, P], F32, name="bank")
+                words = sg_raw[s][:, i, :].bitcast(F32)
+                for g in range(PASSES):
+                    for h in range(2):
+                        nc.tensor.transpose(bank[:, g, h, :], words[:, 2 * P * g + h : 2 * P * (g + 1) : 2], ident[:])
+                banks[s, i] = bank
+
+        def sg_evacuate(s, i):
+            if i == 0:
+                sg_grouped[s] = work.tile([P, 2, PASSES * P * PACK], BF16, name="sg_grouped", align_bytes=64)
+            dst = sg_grouped[s][:, i, :].bitcast(F32).rearrange("p (g r h) -> p g r h", g=PASSES, h=2)
+            nc.scalar.copy(out=dst, in_=banks[s, i][:].rearrange("p g h r -> p g r h"))
+
+        def sg_quantize(s):
+            codes = work.tile([P, 2 * PASSES * P], U32, name="sg_codes", align_bytes=64)
+            scales = work.tile([P, 2 * PASSES * P], U8, name="sg_scales", align_bytes=64)
+            nc.vector.quantize_mx(out=codes[:].bitcast(E5M2), scales=scales[:], in_=sg_grouped[s][:].rearrange("p i c -> p (i c)"))
+            sg_q[s] = (codes, scales)
+
+        def avg_interleave(s):
+            avg_grouped[s] = work.tile([P, PASSES * PAIR, PACK], BF16, name="avg_grouped", align_bytes=64)
+            cols = slice((s % 2) * PAIR, (s % 2 + 1) * PAIR)
+            first, second = avg_grouped[s][:, 0:PAIR, :], avg_grouped[s][:, PAIR : 2 * PAIR, :]
+            interleave(nc.vector.tensor_copy, first, avg_raw[s // 2, 0][:, :, cols], 0, PAIR)
+            interleave(nc.vector.tensor_copy, second, avg_raw[s // 2, 1][:, :, cols], 0, AVG_SPLIT)
+            interleave(nc.scalar.copy, second, avg_raw[s // 2, 1][:, :, cols], AVG_SPLIT, PAIR)
+
+        def avg_quantize(s):
+            codes = work.tile([P, PASSES * PAIR], U32, name="avg_codes", align_bytes=64)
+            scales = work.tile([P, PASSES * PAIR], U8, name="avg_scales", align_bytes=64)
+            nc.vector.quantize_mx(out=codes[:].bitcast(E4M3), scales=scales[:], in_=avg_grouped[s][:].rearrange("p c t -> p (c t)"))
+            avg_q[s] = (codes, scales)
+
+        def direct(s, i):
+            acc[s, i] = sums.tile([P, D], F32, name="acc")
+            codes, scales = sg_q[s]
+            for g in range(PASSES):
+                cols = slice((i * PASSES + g) * P, (i * PASSES + g + 1) * P)
+                nc.tensor.matmul_mx(
+                    out=acc[s, i][:], lhsT=codes[:, cols].bitcast(E5M2), lhsT_scale=scales[:, cols],
+                    rhs=w_codes["cen", g][:].bitcast(E4M3), rhs_scale=w_scales["cen", g][:],
+                    start=(g == 0), stop=False,
+                )
+
+        def shared(s, i):
+            codes, scales = avg_q[s]
+            for g in range(PASSES):
+                cols = slice(g * PAIR + i * P, g * PAIR + (i + 1) * P)
+                nc.tensor.matmul_mx(
+                    out=acc[s, i][:], lhsT=codes[:, cols].bitcast(E4M3), lhsT_scale=scales[:, cols],
+                    rhs=w_codes["cen_grad", g][:].bitcast(E4M3), rhs_scale=w_scales["cen_grad", g][:],
+                    start=False, stop=(g == PASSES - 1),
+                )
+
+        def radial_part(s):
+            for i in range(2):
+                t = 2 * s + i
+                part = work.tile([P, D], F32, name="rad_emb", bufs=4)
+                nc.scalar.activation(out=part[:], in_=emb_raw[t // 4][:, t % 4, :], func=ACT.Copy, scale=rad_inv[:, t : t + 1])
+                rad_emb[s, i] = part
+
+        def finish(s, i):
+            t = 2 * s + i
+            if i == 0:
+                res[s] = keep.tile([P, 2, D], F32, name="res%d" % s)
+            nc.vector.scalar_tensor_tensor(
+                out=res[s][:, i, :], in0=acc[s, i][:], scalar=vec_cols[:, TILES + t : TILES + t + 1], in1=rad_emb[s, i][:],
+                op0=ALU.mult, op1=ALU.subtract,
+            )
+            if s == PAIRS - 1:
+                nc.sync.dma_start(out=out[t * P : (t + 1) * P, :], in_=res[s][:, i, :])
+            elif i == 1:
+                nc.sync.dma_start(out=out[s * PAIR : (s + 1) * PAIR, :].rearrange("(i p) d -> p i d", p=P), in_=res[s][:])
+
+        w_interleave("cen", 0)
+        sg_transpose(0)
+        sg_evacuate(0, 0)
+        sg_evacuate(0, 1)
+        w_quantize("cen", 0)
+        w_interleave("cen", 1)
+        sg_transpose(1)
+        sg_quantize(0)
+        w_quantize("cen", 1)
+        direct(0, 0)
+        direct(0, 1)
+        sg_evacuate(1, 0)
+        sg_evacuate(1, 1)
+        nc.vector.tensor_copy(out=vec_rows[0 : 2 * TILES, :], in_=vec_raw[:])
+        vec_bank = turn.tile([P, PASSES, 2, P], F32, name="bank")
+        nc.tensor.transpose(vec_bank[:, 0, 0, :], vec_rows[:], ident[:])
+        w_interleave("cen_grad", 0)
+        sg_quantize(1)
+        direct(1, 0)
+        direct(1, 1)
+        nc.vector.tensor_copy(out=vec_cols[:], in_=vec_bank[:, 0, 0, 0 : 2 * TILES])
+        w_quantize("cen_grad", 0)
+        nc.vector.tensor_tensor(out=rad_inv[:], in0=vec_cols[:, 0:TILES], in1=vec_cols[:, TILES : 2 * TILES], op=ALU.mult)
+        w_interleave("cen_grad", 1)
+        avg_interleave(0)
+        w_quantize("cen_grad", 1)
+        avg_quantize(0)
+        sg_transpose(2)
+        shared(0, 0)
+        shared(0, 1)
+        avg_interleave(1)
+        sg_evacuate(2, 0)
+        sg_evacuate(2, 1)
+        radial_part(0)
+        avg_quantize(1)
+        shared(1, 0)
+        shared(1, 1)
+        sg_quantize(2)
+        finish(0, 0)
+        avg_interleave(2)
+        finish(0, 1)
+        radial_part(1)
+        avg_quantize(2)
+
+        for s in range(2, PAIRS):
+            ahead = s + 1 < PAIRS
+            if ahead:
+                sg_transpose(s + 1)
+                avg_interleave(s + 1)
+            finish(s - 1, 0)
+            finish(s - 1, 1)
+            for i in range(2):
+                direct(s, i)
+                shared(s, i)
+            if ahead:
+                sg_evacuate(s + 1, 0)
+                sg_evacuate(s + 1, 1)
+            radial_part(s)
+            if ahead:
+                avg_quantize(s + 1)
+                sg_quantize(s + 1)
+        finish(PAIRS - 1, 0)
+        finish(PAIRS - 1, 1)

@@ -24,7 +24,8 @@ PAIR = 2 * P
 PAIRS = U // PAIR
 CHUNK = 2 * PAIR
 RUN = 4
-CEN_SPLIT = 288
+CEN_SPLIT = 384
+GRAD_SPLIT = 256
 AVG_SPLIT = 64
 
 
@@ -32,6 +33,13 @@ def interleave(copy, grouped, raw, c0, c1):
     copy(
         out=grouped[:, c0:c1, :].rearrange("p (c i) t -> p c t i", i=RUN),
         in_=raw[:, :, c0:c1].rearrange("p t (c i) -> p c t i", i=RUN),
+    )
+
+
+def sort_interleave(copy, grouped, raw, i0, i1, m0, m1):
+    copy(
+        out=grouped.rearrange("p (i c m) t -> p i c t m", i=2, m=RUN)[:, i0:i1, m0 // RUN : m1 // RUN],
+        in_=raw.rearrange("p t (c m i) -> p i c t m", i=2, m=RUN)[:, i0:i1, m0 // RUN : m1 // RUN],
     )
 
 
@@ -48,55 +56,57 @@ def tile_ge2e_embedding_gradient_s2_kernel(tc, sim_grad, cen, avg, cen_grad, emb
 
         def load_sg(s):
             sg_raw[s] = keep.tile([P, 2, K], BF16, name="sg_raw%d" % s)
-            nc.sync.dma_start(out=sg_raw[s][:], in_=sim_grad[s * PAIR : (s + 1) * PAIR, :].rearrange("(i p) k -> p i k", p=P))
+            nc.sync.dma_start(out=sg_raw[s][:], in_=sim_grad[s * PAIR : (s + 1) * PAIR, :].rearrange("(p i) k -> p i k", i=2))
 
         def load_w(name, w, g):
             w_raw[name, g] = keep.tile([P, PACK, D], BF16, name="%s_raw%d" % (name, g))
             nc.sync.dma_start(out=w_raw[name, g][:], in_=w[g * K_PASS : (g + 1) * K_PASS, :].rearrange("(p t) d -> p t d", t=PACK))
 
-        def load_avg(c, g):
-            avg_raw[c, g] = keep.tile([P, PACK, CHUNK], BF16, name="avg_raw%d_%d" % (c, g))
-            rows = avg[g * K_PASS : (g + 1) * K_PASS, c * CHUNK : (c + 1) * CHUNK]
-            nc.sync.dma_start(out=avg_raw[c, g][:], in_=rows.rearrange("(p t) u -> p t u", t=PACK))
+        def load_avg(s0, n, g):
+            block = keep.tile([P, PACK, n * PAIR], BF16, name="avg_raw%d_%d" % (s0, g))
+            rows = avg[g * K_PASS : (g + 1) * K_PASS, s0 * PAIR : (s0 + n) * PAIR]
+            nc.sync.dma_start(out=block[:], in_=rows.rearrange("(p t) u -> p t u", t=PACK))
+            for j in range(n):
+                avg_raw[s0 + j, g] = block[:, :, j * PAIR : (j + 1) * PAIR]
 
         def load_emb(c):
-            emb_raw[c] = keep.tile([P, CHUNK // P, D], BF16, name="emb_raw%d" % c)
-            nc.sync.dma_start(out=emb_raw[c][:], in_=emb[c * CHUNK : (c + 1) * CHUNK, :].rearrange("(i p) d -> p i d", p=P))
+            emb_raw[c] = keep.tile([P, 2, 2 * D], BF16, name="emb_raw%d" % c)
+            nc.sync.dma_start(out=emb_raw[c][:], in_=emb[c * CHUNK : (c + 1) * CHUNK, :].rearrange("(s p i) d -> p s (i d)", p=P, i=2))
 
-        vec_raw = keep.tile([2 * TILES, P], BF16)
+        ident = keep.tile([P, P], F32)
+        make_identity(nc, ident[:])
+        vec_rows = keep.tile([P, P], F32)
+        nc.scalar.activation(out=vec_rows[:], in_=ident[:], func=ACT.Copy)
+        vec_words = keep.tile([P, 2 * PAIRS], F32)
+        inv_cols = keep.tile([P, TILES], F32)
+        rad_inv = keep.tile([P, TILES], F32)
+
         load_w("cen", cen, 0)
         load_sg(0)
         load_w("cen", cen, 1)
         load_sg(1)
-        nc.sync.dma_start(out=vec_raw[0:TILES, :], in_=radial.rearrange("(i p) -> i p", p=P))
-        nc.sync.dma_start(out=vec_raw[TILES : 2 * TILES, :], in_=inv_norm.rearrange("(i p) -> i p", p=P))
+        nc.sync.dma_start(out=vec_rows[0:PAIRS, :].bitcast(BF16), in_=radial.rearrange("(s c) -> s c", c=PAIR))
+        nc.sync.dma_start(out=vec_rows[PAIRS : 2 * PAIRS, :].bitcast(BF16), in_=inv_norm.rearrange("(s c) -> s c", c=PAIR))
         load_w("cen_grad", cen_grad, 0)
-        load_avg(0, 0)
+        load_avg(0, 2, 0)
         load_w("cen_grad", cen_grad, 1)
-        load_avg(0, 1)
+        load_avg(0, 2, 1)
         for c in range(U // CHUNK):
             if c > 0:
-                load_avg(c, 0)
-                load_avg(c, 1)
+                load_avg(2 * c, 2, 0)
+                load_avg(2 * c, 2, 1)
                 load_sg(2 * c + 1)
             if 2 * c + 2 < PAIRS:
                 load_sg(2 * c + 2)
             load_emb(c)
 
-        ident = keep.tile([P, P], F32)
-        make_identity(nc, ident[:])
-        vec_rows = keep.tile([P, P], F32)
-        nc.scalar.copy(out=vec_rows[:], in_=ident[:])
-        vec_cols = keep.tile([P, 2 * TILES], F32)
-        rad_inv = keep.tile([P, TILES], F32)
-
         w_codes, w_scales, w_grouped = {}, {}, {}
         banks, sg_grouped, avg_grouped, sg_q, avg_q, acc, res, rad_emb = {}, {}, {}, {}, {}, {}, {}, {}
 
-        def w_interleave(name, g):
+        def w_interleave(name, g, split):
             w_grouped[name, g] = keep.tile([P, D, PACK], BF16, name="%s_grouped%d" % (name, g), align_bytes=64)
-            interleave(nc.vector.tensor_copy, w_grouped[name, g], w_raw[name, g], 0, CEN_SPLIT)
-            interleave(nc.scalar.copy, w_grouped[name, g], w_raw[name, g], CEN_SPLIT, D)
+            interleave(nc.vector.tensor_copy, w_grouped[name, g], w_raw[name, g], 0, split)
+            interleave(nc.scalar.copy, w_grouped[name, g], w_raw[name, g], split, D)
 
         def w_quantize(name, g):
             w_codes[name, g] = keep.tile([P, D], U32, name="%s_codes%d" % (name, g), align_bytes=64)
@@ -130,11 +140,14 @@ def tile_ge2e_embedding_gradient_s2_kernel(tc, sim_grad, cen, avg, cen_grad, emb
 
         def avg_interleave(s):
             avg_grouped[s] = work.tile([P, PASSES * PAIR, PACK], BF16, name="avg_grouped", align_bytes=64)
-            cols = slice((s % 2) * PAIR, (s % 2 + 1) * PAIR)
             first, second = avg_grouped[s][:, 0:PAIR, :], avg_grouped[s][:, PAIR : 2 * PAIR, :]
-            interleave(nc.vector.tensor_copy, first, avg_raw[s // 2, 0][:, :, cols], 0, PAIR)
-            interleave(nc.vector.tensor_copy, second, avg_raw[s // 2, 1][:, :, cols], 0, AVG_SPLIT)
-            interleave(nc.scalar.copy, second, avg_raw[s // 2, 1][:, :, cols], AVG_SPLIT, PAIR)
+            sort_interleave(nc.vector.tensor_copy, first, avg_raw[s, 0], 0, 2, 0, P)
+            if AVG_SPLIT:
+                sort_interleave(nc.vector.tensor_copy, second, avg_raw[s, 1], 0, 1, 0, AVG_SPLIT)
+                sort_interleave(nc.scalar.copy, second, avg_raw[s, 1], 0, 1, AVG_SPLIT, P)
+                sort_interleave(nc.scalar.copy, second, avg_raw[s, 1], 1, 2, 0, P)
+            else:
+                sort_interleave(nc.scalar.copy, second, avg_raw[s, 1], 0, 2, 0, P)
 
         def avg_quantize(s):
             codes = work.tile([P, PASSES * PAIR], U32, name="avg_codes", align_bytes=64)
@@ -167,7 +180,7 @@ def tile_ge2e_embedding_gradient_s2_kernel(tc, sim_grad, cen, avg, cen_grad, emb
             for i in range(2):
                 t = 2 * s + i
                 part = work.tile([P, D], F32, name="rad_emb", bufs=4)
-                nc.scalar.activation(out=part[:], in_=emb_raw[t // 4][:, t % 4, :], func=ACT.Copy, scale=rad_inv[:, t : t + 1])
+                nc.scalar.activation(out=part[:], in_=emb_raw[s // 2][:, s % 2, i * D : (i + 1) * D], func=ACT.Copy, scale=rad_inv[:, t : t + 1])
                 rad_emb[s, i] = part
 
         def finish(s, i):
@@ -175,38 +188,40 @@ def tile_ge2e_embedding_gradient_s2_kernel(tc, sim_grad, cen, avg, cen_grad, emb
             if i == 0:
                 res[s] = keep.tile([P, 2, D], F32, name="res%d" % s)
             nc.vector.scalar_tensor_tensor(
-                out=res[s][:, i, :], in0=acc[s, i][:], scalar=vec_cols[:, TILES + t : TILES + t + 1], in1=rad_emb[s, i][:],
+                out=res[s][:, i, :], in0=acc[s, i][:], scalar=inv_cols[:, t : t + 1], in1=rad_emb[s, i][:],
                 op0=ALU.mult, op1=ALU.subtract,
             )
+            rows = out[s * PAIR : (s + 1) * PAIR, :].rearrange("(p i) d -> p i d", i=2)
             if s == PAIRS - 1:
-                nc.sync.dma_start(out=out[t * P : (t + 1) * P, :], in_=res[s][:, i, :])
+                nc.sync.dma_start(out=rows[:, i, :], in_=res[s][:, i, :])
             elif i == 1:
-                nc.sync.dma_start(out=out[s * PAIR : (s + 1) * PAIR, :].rearrange("(i p) d -> p i d", p=P), in_=res[s][:])
+                nc.sync.dma_start(out=rows, in_=res[s][:])
 
-        w_interleave("cen", 0)
+        w_interleave("cen", 0, CEN_SPLIT)
         sg_transpose(0)
         sg_evacuate(0, 0)
         sg_evacuate(0, 1)
         w_quantize("cen", 0)
-        w_interleave("cen", 1)
+        w_interleave("cen", 1, CEN_SPLIT)
         sg_transpose(1)
+        vec_bank = turn.tile([P, PASSES, 2, P], F32, name="bank")
+        nc.tensor.transpose(vec_bank[:, 0, 0, :], vec_rows[:], ident[:])
         sg_quantize(0)
         w_quantize("cen", 1)
         direct(0, 0)
         direct(0, 1)
         sg_evacuate(1, 0)
         sg_evacuate(1, 1)
-        nc.vector.tensor_copy(out=vec_rows[0 : 2 * TILES, :], in_=vec_raw[:])
-        vec_bank = turn.tile([P, PASSES, 2, P], F32, name="bank")
-        nc.tensor.transpose(vec_bank[:, 0, 0, :], vec_rows[:], ident[:])
-        w_interleave("cen_grad", 0)
+        w_interleave("cen_grad", 0, GRAD_SPLIT)
         sg_quantize(1)
         direct(1, 0)
         direct(1, 1)
-        nc.vector.tensor_copy(out=vec_cols[:], in_=vec_bank[:, 0, 0, 0 : 2 * TILES])
+        nc.vector.tensor_copy(out=vec_words[:], in_=vec_bank[:, 0, 0, 0 : 2 * PAIRS])
         w_quantize("cen_grad", 0)
-        nc.vector.tensor_tensor(out=rad_inv[:], in0=vec_cols[:, 0:TILES], in1=vec_cols[:, TILES : 2 * TILES], op=ALU.mult)
-        w_interleave("cen_grad", 1)
+        vec = vec_words[:].bitcast(BF16)
+        nc.vector.tensor_tensor(out=rad_inv[:], in0=vec[:, 0:TILES], in1=vec[:, TILES : 2 * TILES], op=ALU.mult)
+        nc.vector.tensor_copy(out=inv_cols[:], in_=vec[:, TILES : 2 * TILES])
+        w_interleave("cen_grad", 1, GRAD_SPLIT)
         avg_interleave(0)
         w_quantize("cen_grad", 1)
         avg_quantize(0)

@@ -23,10 +23,13 @@ TILES = U // P
 PAIR = 2 * P
 PAIRS = U // PAIR
 CHUNK = 2 * PAIR
+CHUNKS = U // CHUNK
 RUN = 4
+SGFULL = 0
+LAST = 0
 CEN_SPLIT = 384
 GRAD_SPLIT = 256
-AVG_SPLIT = 64
+AVG_SPLIT = 32
 
 
 def interleave(copy, grouped, raw, c0, c1):
@@ -36,10 +39,10 @@ def interleave(copy, grouped, raw, c0, c1):
     )
 
 
-def sort_interleave(copy, grouped, raw, i0, i1, m0, m1):
+def sort_interleave(copy, grouped, raw, j, m0, m1):
     copy(
-        out=grouped.rearrange("p (i c m) t -> p i c t m", i=2, m=RUN)[:, i0:i1, m0 // RUN : m1 // RUN],
-        in_=raw.rearrange("p t (c m i) -> p i c t m", i=2, m=RUN)[:, i0:i1, m0 // RUN : m1 // RUN],
+        out=grouped.rearrange("p (i c m) t -> p c t m i", i=2, m=2)[:, m0 // 2 : m1 // 2],
+        in_=raw.rearrange("p t (c m j i) -> p j c t m i", m=2, j=2, i=2)[:, j, m0 // 2 : m1 // 2],
     )
 
 
@@ -54,51 +57,60 @@ def tile_ge2e_embedding_gradient_s2_kernel(tc, sim_grad, cen, avg, cen_grad, emb
 
         sg_raw, emb_raw, avg_raw, w_raw = {}, {}, {}, {}
 
-        def load_sg(s):
-            sg_raw[s] = keep.tile([P, 2, K], BF16, name="sg_raw%d" % s)
-            nc.sync.dma_start(out=sg_raw[s][:], in_=sim_grad[s * PAIR : (s + 1) * PAIR, :].rearrange("(p i) k -> p i k", i=2))
+        def load_sg(s0, n):
+            block = keep.tile([P, 2 * n, K], BF16, name="sg_raw%d" % s0)
+            rows = sim_grad[s0 // 2 * CHUNK : (s0 // 2 + 1) * CHUNK, :].rearrange("(p i) k -> p i k", i=4)
+            nc.sync.dma_start(out=block[:], in_=rows[:, s0 % 2 * 2 : s0 % 2 * 2 + 2 * n, :])
+            for j in range(n):
+                sg_raw[s0 + j] = block[:, 2 * j : 2 * j + 2, :]
 
         def load_w(name, w, g):
             w_raw[name, g] = keep.tile([P, PACK, D], BF16, name="%s_raw%d" % (name, g))
             nc.sync.dma_start(out=w_raw[name, g][:], in_=w[g * K_PASS : (g + 1) * K_PASS, :].rearrange("(p t) d -> p t d", t=PACK))
 
-        def load_avg(s0, n, g):
-            block = keep.tile([P, PACK, n * PAIR], BF16, name="avg_raw%d_%d" % (s0, g))
-            rows = avg[g * K_PASS : (g + 1) * K_PASS, s0 * PAIR : (s0 + n) * PAIR]
-            nc.sync.dma_start(out=block[:], in_=rows.rearrange("(p t) u -> p t u", t=PACK))
-            for j in range(n):
-                avg_raw[s0 + j, g] = block[:, :, j * PAIR : (j + 1) * PAIR]
+        def load_avg(c, g):
+            avg_raw[c, g] = keep.tile([P, PACK, CHUNK], BF16, name="avg_raw%d_%d" % (c, g))
+            rows = avg[g * K_PASS : (g + 1) * K_PASS, c * CHUNK : (c + 1) * CHUNK]
+            nc.sync.dma_start(out=avg_raw[c, g][:], in_=rows.rearrange("(p t) u -> p t u", t=PACK))
 
         def load_emb(c):
-            emb_raw[c] = keep.tile([P, 2, 2 * D], BF16, name="emb_raw%d" % c)
-            nc.sync.dma_start(out=emb_raw[c][:], in_=emb[c * CHUNK : (c + 1) * CHUNK, :].rearrange("(s p i) d -> p s (i d)", p=P, i=2))
+            emb_raw[c] = keep.tile([P, 4, D], BF16, name="emb_raw%d" % c)
+            nc.sync.dma_start(out=emb_raw[c][:], in_=emb[c * CHUNK : (c + 1) * CHUNK, :].rearrange("(p i) d -> p i d", i=4))
 
+        vec_rows = keep.tile([P, CHUNK], BF16)
+        nc.gpsimd.memset(vec_rows[:], 0.0)
         ident = keep.tile([P, P], F32)
         make_identity(nc, ident[:])
-        vec_rows = keep.tile([P, P], F32)
-        nc.scalar.activation(out=vec_rows[:], in_=ident[:], func=ACT.Copy)
-        vec_words = keep.tile([P, 2 * PAIRS], F32)
+        vec_words = keep.tile([P, 2 * CHUNKS, 2], F32)
         inv_cols = keep.tile([P, TILES], F32)
         rad_inv = keep.tile([P, TILES], F32)
 
         load_w("cen", cen, 0)
-        load_sg(0)
+        load_sg(0, 1)
         load_w("cen", cen, 1)
-        load_sg(1)
-        nc.sync.dma_start(out=vec_rows[0:PAIRS, :].bitcast(BF16), in_=radial.rearrange("(s c) -> s c", c=PAIR))
-        nc.sync.dma_start(out=vec_rows[PAIRS : 2 * PAIRS, :].bitcast(BF16), in_=inv_norm.rearrange("(s c) -> s c", c=PAIR))
+        load_sg(1, 1)
+        nc.sync.dma_start(out=vec_rows[0:CHUNKS, :], in_=radial.rearrange("(c u) -> c u", u=CHUNK))
+        nc.sync.dma_start(out=vec_rows[CHUNKS : 2 * CHUNKS, :], in_=inv_norm.rearrange("(c u) -> c u", u=CHUNK))
         load_w("cen_grad", cen_grad, 0)
-        load_avg(0, 2, 0)
+        load_avg(0, 0)
         load_w("cen_grad", cen_grad, 1)
-        load_avg(0, 2, 1)
-        for c in range(U // CHUNK):
-            if c > 0:
-                load_avg(2 * c, 2, 0)
-                load_avg(2 * c, 2, 1)
-                load_sg(2 * c + 1)
-            if 2 * c + 2 < PAIRS:
-                load_sg(2 * c + 2)
-            load_emb(c)
+        load_avg(0, 1)
+        if SGFULL:
+            for c in range(1, CHUNKS):
+                load_sg(2 * c, 2)
+                load_emb(c - 1)
+                load_avg(c, 0)
+                load_avg(c, 1)
+            load_emb(CHUNKS - 1)
+        else:
+            for c in range(CHUNKS):
+                if c > 0:
+                    load_avg(c, 0)
+                    load_avg(c, 1)
+                    load_sg(2 * c + 1, 1)
+                if 2 * c + 2 < PAIRS:
+                    load_sg(2 * c + 2, 1)
+                load_emb(c)
 
         w_codes, w_scales, w_grouped = {}, {}, {}
         banks, sg_grouped, avg_grouped, sg_q, avg_q, acc, res, rad_emb = {}, {}, {}, {}, {}, {}, {}, {}
@@ -141,13 +153,9 @@ def tile_ge2e_embedding_gradient_s2_kernel(tc, sim_grad, cen, avg, cen_grad, emb
         def avg_interleave(s):
             avg_grouped[s] = work.tile([P, PASSES * PAIR, PACK], BF16, name="avg_grouped", align_bytes=64)
             first, second = avg_grouped[s][:, 0:PAIR, :], avg_grouped[s][:, PAIR : 2 * PAIR, :]
-            sort_interleave(nc.vector.tensor_copy, first, avg_raw[s, 0], 0, 2, 0, P)
-            if AVG_SPLIT:
-                sort_interleave(nc.vector.tensor_copy, second, avg_raw[s, 1], 0, 1, 0, AVG_SPLIT)
-                sort_interleave(nc.scalar.copy, second, avg_raw[s, 1], 0, 1, AVG_SPLIT, P)
-                sort_interleave(nc.scalar.copy, second, avg_raw[s, 1], 1, 2, 0, P)
-            else:
-                sort_interleave(nc.scalar.copy, second, avg_raw[s, 1], 0, 2, 0, P)
+            sort_interleave(nc.vector.tensor_copy, first, avg_raw[s // 2, 0], s % 2, 0, P)
+            sort_interleave(nc.vector.tensor_copy, second, avg_raw[s // 2, 1], s % 2, 0, AVG_SPLIT)
+            sort_interleave(nc.scalar.copy, second, avg_raw[s // 2, 1], s % 2, AVG_SPLIT, P)
 
         def avg_quantize(s):
             codes = work.tile([P, PASSES * PAIR], U32, name="avg_codes", align_bytes=64)
@@ -180,22 +188,26 @@ def tile_ge2e_embedding_gradient_s2_kernel(tc, sim_grad, cen, avg, cen_grad, emb
             for i in range(2):
                 t = 2 * s + i
                 part = work.tile([P, D], F32, name="rad_emb", bufs=4)
-                nc.scalar.activation(out=part[:], in_=emb_raw[s // 2][:, s % 2, i * D : (i + 1) * D], func=ACT.Copy, scale=rad_inv[:, t : t + 1])
+                nc.scalar.activation(out=part[:], in_=emb_raw[s // 2][:, t % 4, :], func=ACT.Copy, scale=rad_inv[:, t : t + 1])
                 rad_emb[s, i] = part
 
         def finish(s, i):
             t = 2 * s + i
-            if i == 0:
-                res[s] = keep.tile([P, 2, D], F32, name="res%d" % s)
+            c, q = t // 4, t % 4
+            if q == 0:
+                res[c] = keep.tile([P, 4, D], F32, name="res%d" % c)
             nc.vector.scalar_tensor_tensor(
-                out=res[s][:, i, :], in0=acc[s, i][:], scalar=inv_cols[:, t : t + 1], in1=rad_emb[s, i][:],
+                out=res[c][:, q, :], in0=acc[s, i][:], scalar=inv_cols[:, t : t + 1], in1=rad_emb[s, i][:],
                 op0=ALU.mult, op1=ALU.subtract,
             )
-            rows = out[s * PAIR : (s + 1) * PAIR, :].rearrange("(p i) d -> p i d", i=2)
-            if s == PAIRS - 1:
-                nc.sync.dma_start(out=rows[:, i, :], in_=res[s][:, i, :])
-            elif i == 1:
-                nc.sync.dma_start(out=rows, in_=res[s][:])
+            rows = out[c * CHUNK : (c + 1) * CHUNK, :].rearrange("(p i) d -> p i d", i=4)
+            if c < CHUNKS - 1:
+                if q == 3:
+                    nc.sync.dma_start(out=rows, in_=res[c][:])
+            elif q == 1 or (q == 3 and LAST):
+                nc.sync.dma_start(out=rows[:, q - 1 : q + 1, :], in_=res[c][:, q - 1 : q + 1, :])
+            elif q > 1 and not LAST:
+                nc.sync.dma_start(out=rows[:, q, :], in_=res[c][:, q, :])
 
         w_interleave("cen", 0, CEN_SPLIT)
         sg_transpose(0)
@@ -205,7 +217,8 @@ def tile_ge2e_embedding_gradient_s2_kernel(tc, sim_grad, cen, avg, cen_grad, emb
         w_interleave("cen", 1, CEN_SPLIT)
         sg_transpose(1)
         vec_bank = turn.tile([P, PASSES, 2, P], F32, name="bank")
-        nc.tensor.transpose(vec_bank[:, 0, 0, :], vec_rows[:], ident[:])
+        for j in range(2):
+            nc.tensor.transpose(vec_bank[:, 0, j, :], vec_rows[:].bitcast(F32)[:, j : 2 * P : 2], ident[:])
         sg_quantize(0)
         w_quantize("cen", 1)
         direct(0, 0)
@@ -216,9 +229,9 @@ def tile_ge2e_embedding_gradient_s2_kernel(tc, sim_grad, cen, avg, cen_grad, emb
         sg_quantize(1)
         direct(1, 0)
         direct(1, 1)
-        nc.vector.tensor_copy(out=vec_words[:], in_=vec_bank[:, 0, 0, 0 : 2 * PAIRS])
+        nc.vector.tensor_copy(out=vec_words[:], in_=vec_bank[:, 0, :, 0 : 2 * CHUNKS].rearrange("p j r -> p r j"))
         w_quantize("cen_grad", 0)
-        vec = vec_words[:].bitcast(BF16)
+        vec = vec_words[:].rearrange("p r j -> p (r j)").bitcast(BF16)
         nc.vector.tensor_tensor(out=rad_inv[:], in0=vec[:, 0:TILES], in1=vec[:, TILES : 2 * TILES], op=ALU.mult)
         nc.vector.tensor_copy(out=inv_cols[:], in_=vec[:, TILES : 2 * TILES])
         w_interleave("cen_grad", 1, GRAD_SPLIT)

from contextlib import ExitStack

import concourse.mybir as mybir
from concourse.masks import make_identity

U, K, D = 2048, 1024, 512
FLOPS = 2 * 2 * U * K * D

F32 = mybir.dt.float32
BF16 = mybir.dt.bfloat16
U32 = mybir.dt.uint32
U8 = mybir.dt.uint8
E4M3 = mybir.dt.float8_e4m3fn_x4
E5M2 = mybir.dt.float8_e5m2_x4
ALU = mybir.AluOpType
ACT = mybir.ActivationFunctionType

P = 128
PACK = 4
K_PASS = P * PACK
PASSES = K // K_PASS
TILES = U // P
PAIR = 2 * P
PAIRS = U // PAIR
CHUNK = 2 * PAIR
CHUNKS = U // CHUNK
RUN = 4
SGFULL = 0
LAST = 0
CEN_SPLIT = 384
GRAD_SPLIT = 256
AVG_SPLIT = 32


def interleave(copy, grouped, raw, c0, c1):
    copy(
        out=grouped[:, c0:c1, :].rearrange("p (c i) t -> p c t i", i=RUN),
        in_=raw[:, :, c0:c1].rearrange("p t (c i) -> p c t i", i=RUN),
    )


def sort_interleave(copy, grouped, raw, j, m0, m1):
    copy(
        out=grouped.rearrange("p (i c m) t -> p c t m i", i=2, m=2)[:, m0 // 2 : m1 // 2],
        in_=raw.rearrange("p t (c m j i) -> p j c t m i", m=2, j=2, i=2)[:, j, m0 // 2 : m1 // 2],
    )


def tile_ge2e_embedding_gradient_s2_kernel(tc, sim_grad, cen, avg, cen_grad, emb, radial, inv_norm, out):
    nc = tc.nc
    with ExitStack() as ctx:
        keep = ctx.enter_context(tc.tile_pool(name="keep", bufs=1))
        work = ctx.enter_context(tc.tile_pool(name="work", bufs=3))
        turn = ctx.enter_context(tc.psum_pool(name="turn", bufs=4))
        sums = ctx.enter_context(tc.psum_pool(name="sums", bufs=4))
        ctx.enter_context(tc.manual_schedule())

        sg_raw, emb_raw, avg_raw, w_raw = {}, {}, {}, {}

        def load_sg(s0, n):
            block = keep.tile([P, 2 * n, K], BF16, name="sg_raw%d" % s0)
            rows = sim_grad[s0 // 2 * CHUNK : (s0 // 2 + 1) * CHUNK, :].rearrange("(p i) k -> p i k", i=4)
            nc.sync.dma_start(out=block[:], in_=rows[:, s0 % 2 * 2 : s0 % 2 * 2 + 2 * n, :])
            for j in range(n):
                sg_raw[s0 + j] = block[:, 2 * j : 2 * j + 2, :]

        def load_w(name, w, g):
            w_raw[name, g] = keep.tile([P, PACK, D], BF16, name="%s_raw%d" % (name, g))
            nc.sync.dma_start(out=w_raw[name, g][:], in_=w[g * K_PASS : (g + 1) * K_PASS, :].rearrange("(p t) d -> p t d", t=PACK))

        def load_avg(c, g):
            avg_raw[c, g] = keep.tile([P, PACK, CHUNK], BF16, name="avg_raw%d_%d" % (c, g))
            rows = avg[g * K_PASS : (g + 1) * K_PASS, c * CHUNK : (c + 1) * CHUNK]
            nc.sync.dma_start(out=avg_raw[c, g][:], in_=rows.rearrange("(p t) u -> p t u", t=PACK))

        def load_emb(c):
            emb_raw[c] = keep.tile([P, 4, D], BF16, name="emb_raw%d" % c)
            nc.sync.dma_start(out=emb_raw[c][:], in_=emb[c * CHUNK : (c + 1) * CHUNK, :].rearrange("(p i) d -> p i d", i=4))

        vec_rows = keep.tile([P, CHUNK], BF16)
        nc.gpsimd.memset(vec_rows[:], 0.0)
        ident = keep.tile([P, P], F32)
        make_identity(nc, ident[:])
        vec_words = keep.tile([P, 2 * CHUNKS, 2], F32)
        inv_cols = keep.tile([P, TILES], F32)
        rad_inv = keep.tile([P, TILES], F32)

        load_w("cen", cen, 0)
        load_sg(0, 1)
        load_w("cen", cen, 1)
        load_sg(1, 1)
        nc.sync.dma_start(out=vec_rows[0:CHUNKS, :], in_=radial.rearrange("(c u) -> c u", u=CHUNK))
        nc.sync.dma_start(out=vec_rows[CHUNKS : 2 * CHUNKS, :], in_=inv_norm.rearrange("(c u) -> c u", u=CHUNK))
        load_w("cen_grad", cen_grad, 0)
        load_avg(0, 0)
        load_w("cen_grad", cen_grad, 1)
        load_avg(0, 1)
        if SGFULL:
            for c in range(1, CHUNKS):
                load_sg(2 * c, 2)
                load_emb(c - 1)
                load_avg(c, 0)
                load_avg(c, 1)
            load_emb(CHUNKS - 1)
        else:
            for c in range(CHUNKS):
                if c > 0:
                    load_avg(c, 0)
                    load_avg(c, 1)
                    load_sg(2 * c + 1, 1)
                if 2 * c + 2 < PAIRS:
                    load_sg(2 * c + 2, 1)
                load_emb(c)

        w_codes, w_scales, w_grouped = {}, {}, {}
        banks, sg_grouped, avg_grouped, sg_q, avg_q, acc, res, rad_emb = {}, {}, {}, {}, {}, {}, {}, {}

        def w_interleave(name, g, split):
            w_grouped[name, g] = keep.tile([P, D, PACK], BF16, name="%s_grouped%d" % (name, g), align_bytes=64)
            interleave(nc.vector.tensor_copy, w_grouped[name, g], w_raw[name, g], 0, split)
            interleave(nc.scalar.copy, w_grouped[name, g], w_raw[name, g], split, D)

        def w_quantize(name, g):
            w_codes[name, g] = keep.tile([P, D], U32, name="%s_codes%d" % (name, g), align_bytes=64)
            w_scales[name, g] = keep.tile([P, D], U8, name="%s_scales%d" % (name, g), align_bytes=64)
            nc.vector.quantize_mx(
                out=w_codes[name, g][:].bitcast(E4M3),
                scales=w_scales[name, g][:],
                in_=w_grouped[name, g][:].rearrange("p d t -> p (d t)"),
            )

        def sg_transpose(s):
            for i in range(2):
                bank = turn.tile([P, PASSES, 2, P], F32, name="bank")
                words = sg_raw[s][:, i, :].bitcast(F32)
                for g in range(PASSES):
                    for h in range(2):
                        nc.tensor.transpose(bank[:, g, h, :], words[:, 2 * P * g + h : 2 * P * (g + 1) : 2], ident[:])
                banks[s, i] = bank

        def sg_evacuate(s, i):
            if i == 0:
                sg_grouped[s] = work.tile([P, 2, PASSES * P * PACK], BF16, name="sg_grouped", align_bytes=64)
            dst = sg_grouped[s][:, i, :].bitcast(F32).rearrange("p (g r h) -> p g r h", g=PASSES, h=2)
            nc.scalar.copy(out=dst, in_=banks[s, i][:].rearrange("p g h r -> p g r h"))

        def sg_quantize(s):
            codes = work.tile([P, 2 * PASSES * P], U32, name="sg_codes", align_bytes=64)
            scales = work.tile([P, 2 * PASSES * P], U8, name="sg_scales", align_bytes=64)
            nc.vector.quantize_mx(out=codes[:].bitcast(E5M2), scales=scales[:], in_=sg_grouped[s][:].rearrange("p i c -> p (i c)"))
            sg_q[s] = (codes, scales)

        def avg_interleave(s):
            avg_grouped[s] = work.tile([P, PASSES * PAIR, PACK], BF16, name="avg_grouped", align_bytes=64)
            first, second = avg_grouped[s][:, 0:PAIR, :], avg_grouped[s][:, PAIR : 2 * PAIR, :]
            sort_interleave(nc.vector.tensor_copy, first, avg_raw[s // 2, 0], s % 2, 0, P)
            sort_interleave(nc.vector.tensor_copy, second, avg_raw[s // 2, 1], s % 2, 0, AVG_SPLIT)
            sort_interleave(nc.scalar.copy, second, avg_raw[s // 2, 1], s % 2, AVG_SPLIT, P)

        def avg_quantize(s):
            codes = work.tile([P, PASSES * PAIR], U32, name="avg_codes", align_bytes=64)
            scales = work.tile([P, PASSES * PAIR], U8, name="avg_scales", align_bytes=64)
            nc.vector.quantize_mx(out=codes[:].bitcast(E4M3), scales=scales[:], in_=avg_grouped[s][:].rearrange("p c t -> p (c t)"))
            avg_q[s] = (codes, scales)

        def direct(s, i):
            acc[s, i] = sums.tile([P, D], F32, name="acc")
            codes, scales = sg_q[s]
            for g in range(PASSES):
                cols = slice((i * PASSES + g) * P, (i * PASSES + g + 1) * P)
                nc.tensor.matmul_mx(
                    out=acc[s, i][:], lhsT=codes[:, cols].bitcast(E5M2), lhsT_scale=scales[:, cols],
                    rhs=w_codes["cen", g][:].bitcast(E4M3), rhs_scale=w_scales["cen", g][:],
                    start=(g == 0), stop=False,
                )

        def shared(s, i):
            codes, scales = avg_q[s]
            for g in range(PASSES):
                cols = slice(g * PAIR + i * P, g * PAIR + (i + 1) * P)
                nc.tensor.matmul_mx(
                    out=acc[s, i][:], lhsT=codes[:, cols].bitcast(E4M3), lhsT_scale=scales[:, cols],
                    rhs=w_codes["cen_grad", g][:].bitcast(E4M3), rhs_scale=w_scales["cen_grad", g][:],
                    start=False, stop=(g == PASSES - 1),
                )

        def radial_part(s):
            for i in range(2):
                t = 2 * s + i
                part = work.tile([P, D], F32, name="rad_emb", bufs=4)
                nc.scalar.activation(out=part[:], in_=emb_raw[s // 2][:, t % 4, :], func=ACT.Copy, scale=rad_inv[:, t : t + 1])
                rad_emb[s, i] = part

        def finish(s, i):
            t = 2 * s + i
            c, q = t // 4, t % 4
            if q == 0:
                res[c] = keep.tile([P, 4, D], F32, name="res%d" % c)
            nc.vector.scalar_tensor_tensor(
                out=res[c][:, q, :], in0=acc[s, i][:], scalar=inv_cols[:, t : t + 1], in1=rad_emb[s, i][:],
                op0=ALU.mult, op1=ALU.subtract,
            )
            rows = out[c * CHUNK : (c + 1) * CHUNK, :].rearrange("(p i) d -> p i d", i=4)
            if c < CHUNKS - 1:
                if q == 3:
                    nc.sync.dma_start(out=rows, in_=res[c][:])
            elif q == 1 or (q == 3 and LAST):
                nc.sync.dma_start(out=rows[:, q - 1 : q + 1, :], in_=res[c][:, q - 1 : q + 1, :])
            elif q > 1 and not LAST:
                nc.sync.dma_start(out=rows[:, q, :], in_=res[c][:, q, :])

        w_interleave("cen", 0, CEN_SPLIT)
        sg_transpose(0)
        sg_evacuate(0, 0)
        sg_evacuate(0, 1)
        w_quantize("cen", 0)
        w_interleave("cen", 1, CEN_SPLIT)
        sg_transpose(1)
        vec_bank = turn.tile([P, PASSES, 2, P], F32, name="bank")
        for j in range(2):
            nc.tensor.transpose(vec_bank[:, 0, j, :], vec_rows[:].bitcast(F32)[:, j : 2 * P : 2], ident[:])
        sg_quantize(0)
        w_quantize("cen", 1)
        direct(0, 0)
        direct(0, 1)
        sg_evacuate(1, 0)
        sg_evacuate(1, 1)
        w_interleave("cen_grad", 0, GRAD_SPLIT)
        sg_quantize(1)
        direct(1, 0)
        direct(1, 1)
        nc.vector.tensor_copy(out=vec_words[:], in_=vec_bank[:, 0, :, 0 : 2 * CHUNKS].rearrange("p j r -> p r j"))
        w_quantize("cen_grad", 0)
        vec = vec_words[:].rearrange("p r j -> p (r j)").bitcast(BF16)
        nc.vector.tensor_tensor(out=rad_inv[:], in0=vec[:, 0:TILES], in1=vec[:, TILES : 2 * TILES], op=ALU.mult)
        nc.vector.tensor_copy(out=inv_cols[:], in_=vec[:, TILES : 2 * TILES])
        w_interleave("cen_grad", 1, GRAD_SPLIT)
        avg_interleave(0)
        w_quantize("cen_grad", 1)
        avg_quantize(0)
        sg_transpose(2)
        shared(0, 0)
        shared(0, 1)
        avg_interleave(1)
        sg_evacuate(2, 0)
        sg_evacuate(2, 1)
        radial_part(0)
        avg_quantize(1)
        shared(1, 0)
        shared(1, 1)
        sg_quantize(2)
        finish(0, 0)
        avg_interleave(2)
        finish(0, 1)
        radial_part(1)
        avg_quantize(2)

        for s in range(2, PAIRS):
            ahead = s + 1 < PAIRS
            if ahead:
                sg_transpose(s + 1)
                avg_interleave(s + 1)
            finish(s - 1, 0)
            finish(s - 1, 1)
            for i in range(2):
                direct(s, i)
                shared(s, i)
            if ahead:
                sg_evacuate(s + 1, 0)
                sg_evacuate(s + 1, 1)
            radial_part(s)
            if ahead:
                avg_quantize(s + 1)
                sg_quantize(s + 1)
        finish(PAIRS - 1, 0)
        finish(PAIRS - 1, 1)
